import numpy as np, ml_dtypes
CORES = [2,3,42,43,82,83,122,123]
N = 8
import mx_ref
BF = ml_dtypes.bfloat16
def entries(a):
    return np.ascontiguousarray(a.T).reshape(-1)
def table(e):
    return np.ascontiguousarray(np.reshape(e, (-1, 16)).T).astype(np.int32)
def gentries(a):
    return np.ascontiguousarray(a.reshape(8, 16, -1).transpose(0, 2, 1)).reshape(8, -1)
def gtable(e):
    e = np.asarray(e); return np.ascontiguousarray(e.reshape(8, -1, 16).transpose(0, 2, 1)).reshape(128, -1).astype(np.int32)
def cols(t, e):
    v = np.concatenate([t.reshape(128, -1, 4), np.zeros((128, 1, 4), BF)], axis=1)
    return np.ascontiguousarray(v[:, e]).reshape(128, -1)
def gpick(z, e):
    return np.concatenate([z[16 * g:16 * g + 16][:, e[g]] for g in range(8)])
def tile(rs):
    return np.stack(rs, axis=2).reshape(128, -1).astype(BF)
def cut(t, i, w=512):
    return t[:, w * i:w * i + w]
def f(rng, *shape):
    return mx_ref.flush((rng.standard_normal(shape, dtype=np.float32) * np.exp2(rng.integers(-2, 3, shape[:-1] + (1,)))).astype(BF))
def wide(rng, *shape, cols=0):
    v = rng.standard_normal(shape, dtype=np.float32) * np.exp2(rng.integers(-12, 13, shape)).astype(np.float32)
    if cols: v *= np.repeat(np.exp2(rng.integers(-cols, cols + 1, shape[:-2] + (1, shape[-1] // 4))) * (rng.random(shape[:-2] + (1, shape[-1] // 4)) > 0.0625), 4, axis=-1).astype(np.float32)
    return mx_ref.flush(v.astype(BF))
T, CAPP, KH, O = 512, 64, 512, 1
def lists(rng, kind="plain"):
    g = np.full((N, N * CAPP), -1)
    for s in range(N):
        for d in range(N):
            if d == s: continue
            n = rng.integers(0, CAPP + 1)
            if kind in ("foreign", "one"): n = CAPP
            if kind == "own": n = CAPP if d == (s + 1) % N else 0
            g[s, d * CAPP + rng.permutation(CAPP)[:n]] = rng.permutation(T)[:n] if n == CAPP else rng.integers(0, T, n)
    p = []
    for r in range(N):
        near = np.arange(T)
        far = T + np.flatnonzero(g[:, r * CAPP:(r + 1) * CAPP].reshape(-1) >= 0)
        if len(far) == 0: far = near
        e = np.where(rng.random((8, KH)) < 0.5, rng.choice(near, (8, KH)), rng.choice(far, (8, KH)))
        if kind == "agree": e = np.repeat(e[:1], 8, axis=0)
        if kind == "foreign": e = rng.choice(far, (8, KH))
        if kind == "own": e = rng.choice(near, (8, KH))
        if kind == "one":
            k = rng.permutation(np.concatenate([rng.permutation(near)[:4], rng.permutation(far)[:4]]))
            e = np.repeat(k[:, None], KH, axis=1)
        p.append(gtable(e))
    return {"snd": np.stack([table(g[s]) for s in range(N)]), "pk": np.stack(p)}
def setup_inputs(rng):
    return {"x": f(rng, N, 128, 4 * T), "w": f(rng, N, 128, 2048), "v": f(rng, N, 128, O * 512), **lists(rng)}
def setup_inputs_agree(rng):
    return {**setup_inputs(rng), **lists(rng, "agree")}
def setup_inputs_foreign(rng):
    return {**setup_inputs(rng), **lists(rng, "foreign")}
def setup_inputs_own(rng):
    return {**setup_inputs(rng), **lists(rng, "own")}
def setup_inputs_one(rng):
    return {**setup_inputs(rng), **lists(rng, "one")}
def setup_inputs_spread(rng):
    d = setup_inputs(rng); d["x"] = wide(rng, N, 128, 4 * T, cols=8); return d
def check_inputs(d):
    b = []
    g = np.stack([entries(d["snd"][s]) for s in range(N)])
    for r in range(N):
        if g[r].min() < -1 or g[r].max() >= T or (g[r, r * CAPP:(r + 1) * CAPP] != -1).any(): b.append("snd")
        e = gentries(d["pk"][r])
        if e.min() < 0 or e.max() >= T + N * CAPP: b.append("pk")
        else:
            used = g[:, r * CAPP:(r + 1) * CAPP].reshape(-1) >= 0
            if not used[e[e >= T] - T].all(): b.append("pk")
    return b
def reference(x, w, v, snd, pk):
    y = np.zeros((N, 128, O * KH), np.float32)
    for r in range(N):
        t = np.concatenate([x[r]] + [cols(x[s], entries(snd[s])[r * CAPP:(r + 1) * CAPP]) for s in range(N)], axis=1)
        q = mx_ref.quantize(np.ascontiguousarray(t))
        e = gentries(pk[r])
        rs = []
        for b in range(4):
            z = mx_ref.matmul(mx_ref.quantize(np.ascontiguousarray(cut(w[r], b))), q)
            rs.append(np.maximum(gpick(z, e), np.float32(0)) * np.float32(0.05))
        h = mx_ref.quantize(np.ascontiguousarray(tile(rs)))
        for o in range(O): y[r][:, KH * o:KH * o + KH] = mx_ref.matmul(mx_ref.quantize(np.ascontiguousarray(cut(v[r], o))), h)
    return {"y": y}

@@ -1,0 +1,233 @@
+from concourse.bass import DstId, RemoteDMATransfer
+from concourse.mybir import dt, AluOpType, ActivationFunctionType
+
+N, W, CAP, PICKS = 8, 512, 64, 512
+PAD = 16
+CODES, BYTE = "float8_e4m3fn_x4", "uint8"
+SCRATCH = {
+    "lst": ("sbuf", [128, 32], "int32"),
+    "pkl": ("sbuf", [128, 32], "int32"),
+    "pko": ("sbuf", [128, 32], "uint16"),
+    "xs": ("sbuf", [128, PAD + 4 * W], "bfloat16"),
+    "ws": ("sbuf", [128, 2048], "bfloat16"),
+    "vs": ("sbuf", [128, 512], "bfloat16"),
+    "gath": ("sbuf", [128, 4 * 7 * CAP], "bfloat16"),
+    "sq": ("sbuf", [128, 7 * CAP], CODES),
+    "sp": ("sbuf", [128, 7 * CAP], BYTE),
+    "cq": ("sbuf", [128, W + 7 * CAP], CODES),
+    "cp": ("sbuf", [128, W + 7 * CAP], BYTE),
+    "wq": ("sbuf", [128, 512], CODES),
+    "wp": ("sbuf", [128, 512], BYTE),
+    "vq": ("sbuf", [128, 128], CODES),
+    "vp": ("sbuf", [128, 128], BYTE),
+    "h": ("sbuf", [128, 4 * PICKS], "bfloat16"),
+    "hq": ("sbuf", [128, PICKS], CODES),
+    "hp": ("sbuf", [128, PICKS], BYTE),
+    "ys": ("sbuf", [128, PICKS], "float32"),
+    "ps": ("psum", [128, 4096], "float32"),
+}
+for _t in range(4):
+    SCRATCH["off%d" % _t] = ("sbuf", [128, 32], "uint16")
+    SCRATCH["res%d" % _t] = ("sbuf", [128, W + N * CAP], "bfloat16")
+SEMAPHORES = (["lst", "xin", "pkin", "win", "vin", "pad", "wqd", "xqd", "vqd", "pkd", "loc"]
+              + [k + "%d" % i for k in ("off", "gat", "sqd", "fill", "mo", "ro", "ms", "rs", "hg", "hq", "my", "cy", "out",
+                                        "arr", "ma", "mb", "mc", "ra", "rb", "rc") for i in range(4)])
+
+
+def mask_of(engines):
+    return sum(1 << e for e in engines)
+
+
+def groups_of(T, topo):
+    out = {}
+    for r, c in enumerate(T.cores):
+        out.setdefault(topo.chip(c), []).append(r)
+    return [out[k] for k in sorted(out, key=lambda k: out[k][0])]
+
+
+def ring(rank, step, T, topo):
+    groups = groups_of(T, topo)
+    mine = [i for i, q in enumerate(groups) if rank in q][0]
+    around = [(mine + step * k) % len(groups) for k in range(1, len(groups))]
+    near = [i for i in around if topo.same_plane(topo.chip(T.cores[rank]), topo.chip(T.cores[groups[i][0]]))]
+    return [i for i in around if i not in near] + near
+
+
+def place(dst, src, T, topo):
+    groups = groups_of(T, topo)
+    i = [n for n, q in enumerate(groups) if src in q][0]
+    if dst in groups[i]:
+        return W, i
+    return W + CAP + 2 * CAP * ring(dst, -1, T, topo).index(i) + CAP * groups[i].index(src), i
+
+
+def send(g, core, me, dests, at, T, topo):
+    far = [d for d in dests if topo.chip(T.cores[d]) != topo.chip(core)]
+    away = topo.engines(core, T.cores[far[0]])
+    share, total = len(away) // len(far), 0
+    for buf, land in (("sq", "cq"), ("sp", "cp")):
+        trs = []
+        for d in dests:
+            if d in far:
+                k = far.index(d)
+                eng = away[k * share:(k + 1) * share]
+            else:
+                eng = [e for e in topo.engines(core, T.cores[d]) if e not in away][:len(away)]
+            col, i = place(d, me, T, topo)
+            a, b = T[buf][:, at[d]:at[d] + CAP], T[land][:, col:col + CAP]
+            if buf == "sq":
+                a, b = a.bitcast(dt.uint8), b.bitcast(dt.uint8)
+            rid, pid, _ = topo.addr(T.cores[d])
+            trs.append(RemoteDMATransfer(dst_ids=[DstId(rid=rid, pnc=pid)], dma_engine_mask=mask_of(eng),
+                                         remote_sem=T.sem["arr%d" % i], src=a, dst=b))
+            total += len(eng)
+        g.remote_dma_fused(trs, local_sem=T.sem.loc)
+    return total
+
+
+def rank_program(g, core, T, topo):
+    rank = T.rank_of(core)
+    if rank is None:
+        return
+    S, V, A, E, Y = T.sem, g.vector, g.scalar, g.tensor, g.sync
+    COPY, RELU = ActivationFunctionType.Copy, ActivationFunctionType.Relu
+    groups = groups_of(T, topo)
+    mine = [i for i, q in enumerate(groups) if rank in q][0]
+    mate = [d for d in groups[mine] if d != rank][0]
+    steps = [list(groups[i]) for i in ring(rank, 1, T, topo)]
+    steps[1].append(mate)
+    at, pieces, col = {}, [], 0
+    for dests in steps:
+        runs, lo = [], col
+        for d in sorted(dests):
+            at[d] = col
+            if runs and runs[-1][1] == d:
+                runs[-1][1] = d + 1
+            else:
+                runs.append([d, d + 1, col])
+            col += CAP
+        pieces.append((runs, lo, col))
+
+    for q in range(8):
+        (Y if q < 3 else A).dma_start(T.lst[16 * q:16 * q + 16, :], T.snd[:, :]).then_inc(S.lst, 16)
+    Y.dma_start(T.xs[:, PAD:PAD + 4 * W], T.x[:, :]).then_inc(S.xin, 16)
+    Y.dma_start(T.ws[:], T.w[:, :]).then_inc(S.win, 16)
+    Y.dma_start(T.pkl[:], T.pk[:, :]).then_inc(S.pkin, 16)
+    Y.dma_start(T.vs[:], T.v[:, :]).then_inc(S.vin, 16)
+
+    V.memset(T.xs[:, 0:PAD], 0.0).then_inc(S.pad, 1)
+    V.wait_ge(S.lst, 128)
+    for t in (2, 0, 3, 1):
+        V.tensor_scalar(T["off%d" % t][:], T.lst[:], 4.0, float(PAD + t), AluOpType.mult, AluOpType.add).then_inc(S["off%d" % t], 1)
+    for b in range(4):
+        V.memset(T["res%d" % b][:, W + CAP * rank:W + CAP * rank + CAP], 0.0).then_inc(S["fill%d" % b], 1)
+
+    for q, ts in ((V, (0, 1)), (A, (2, 3))):
+        q.wait_ge(S.pad, 1)
+        q.wait_ge(S.xin, 16)
+        for t in ts:
+            q.wait_ge(S["off%d" % t], 1)
+    sent = 0
+    for k, dests in enumerate(steps):
+        runs, lo, hi = pieces[k]
+        for t in range(4):
+            for d0, d1, c in runs:
+                out = T.gath[:, 4 * c + t:4 * (c + CAP * (d1 - d0)):4]
+                src = T.xs[:, 0:PAD + 4 * W].indirect(T["off%d" % t][:, 4 * d0:4 * d1])
+                if t < 2:
+                    V.tensor_copy(out, src).then_inc(S["gat%d" % k], 1)
+                else:
+                    A.activation(out, src, COPY).then_inc(S["gat%d" % k], 1)
+        V.wait_ge(S["gat%d" % k], 4 * len(runs))
+        V.quantize_mx(T.sq[:, lo:hi], T.sp[:, lo:hi], T.gath[:, 4 * lo:4 * hi]).then_inc(S["sqd%d" % k], 1)
+        g.wait_ge(S["sqd%d" % k], 1)
+        sent += send(g, core, rank, dests, at, T, topo)
+    g.wait_ge(S.loc, sent)
+
+    V.wait_ge(S.win, 16)
+    V.quantize_mx(T.wq[:], T.wp[:], T.ws[:]).then_inc(S.wqd, 1)
+    V.quantize_mx(T.cq[:, 0:W], T.cp[:, 0:W], T.xs[:, PAD:PAD + 4 * W]).then_inc(S.xqd, 1)
+    V.wait_ge(S.vin, 16)
+    V.quantize_mx(T.vq[:], T.vp[:], T.vs[:]).then_inc(S.vqd, 1)
+    V.wait_ge(S.pkin, 16)
+    V.tensor_copy(T.pko[:], T.pkl[:]).then_inc(S.pkd, 1)
+
+    def product(b, bank, lo, hi, done):
+        E.matmul_mx(T.ps[:, 512 * bank:512 * bank + hi - lo], T.wq[:, 128 * b:128 * b + 128], T.wp[:, 128 * b:128 * b + 128],
+                    T.cq[:, lo:hi], T.cp[:, lo:hi], True, True).then_inc(S["%s%d" % (done, b)], 1)
+
+    def keep(b, bank, skip, lo, n, made, done):
+        q = V if b < 2 else A
+        q.wait_ge(S["%s%d" % (made, b)], 1)
+        src, out = T.ps[:, 512 * bank + skip:512 * bank + skip + n], T["res%d" % b][:, lo:lo + n]
+        if b < 2:
+            V.tensor_scalar(out, src, 0.0, 0.05, AluOpType.max, AluOpType.mult).then_inc(S["%s%d" % (done, b)], 1)
+        else:
+            A.activation(out, src, RELU, scale=0.05).then_inc(S["%s%d" % (done, b)], 1)
+
+    BS = (0, 2, 1, 3)
+    E.wait_ge(S.wqd, 1)
+    E.wait_ge(S.xqd, 1)
+    for b in BS:
+        product(b, b, 0, W, "mo")
+        keep(b, b, 0, 0, W, "mo", "ro")
+    away = topo.engines(core, T.cores[groups[mine - 1][0]])
+    E.wait_ge(S["arr%d" % mine], 2 * len(away))
+    for b in BS:
+        product(b, 4 + b, W - CAP, W + CAP, "ms")
+        keep(b, 4 + b, CAP, W + CAP * mate, CAP, "ms", "rs")
+    for n, i in enumerate(ring(rank, -1, T, topo)):
+        E.wait_ge(S["arr%d" % i], 2 * len(away))
+        lo = W + CAP + 2 * CAP * n
+        for b in BS:
+            bank = (0, 4, 0)[n] + b
+            E.wait_ge(S["%s%d" % (("ro", "rs", "ra")[n], b)], 1)
+            product(b, bank, lo, lo + 2 * CAP, ("ma", "mb", "mc")[n])
+            keep(b, bank, 0, W + CAP * groups[i][0], 2 * CAP, ("ma", "mb", "mc")[n], ("ra", "rb", "rc")[n])
+
+    def ready(q, b):
+        for k in ("fill", "ro", "rs", "ra", "rb", "rc"):
+            q.wait_ge(S["%s%d" % (k, b)], 1)
+
+    def pick(q, b, lo, hi, done):
+        out = T.h[:, 4 * lo + b:4 * hi:4]
+        idx = T["res%d" % b][:, 0:W + N * CAP].indirect(T.pko[:, lo // 16:hi // 16])
+        if q is V:
+            V.tensor_copy(out, idx).then_inc(done, 1)
+        else:
+            A.activation(out, idx, COPY).then_inc(done, 1)
+
+    H, M = 320, 416
+    V.wait_ge(S.pkd, 1)
+    A.wait_ge(S.pkd, 1)
+    for q, bs in ((V, (0, 1)), (A, (2, 3))):
+        for b in bs:
+            ready(q, b)
+            pick(q, b, 0, H, S.hg0)
+    pick(V, 0, H, PICKS, S.hg1)
+    V.wait_ge(S.hg0, 4)
+    V.quantize_mx(T.hq[:, 0:H], T.hp[:, 0:H], T.h[:, 0:4 * H]).then_inc(S.hq0, 1)
+    pick(V, 1, H, M, S.hg1)
+    pick(A, 2, H, PICKS, S.hg1)
+    pick(A, 3, H, PICKS, S.hg1)
+    ready(A, 1)
+    pick(A, 1, M, PICKS, S.hg1)
+    V.wait_ge(S.hg1, 5)
+    V.quantize_mx(T.hq[:, H:PICKS], T.hp[:, H:PICKS], T.h[:, 4 * H:4 * PICKS]).then_inc(S.hq1, 1)
+    E.wait_ge(S.vqd, 1)
+    for n, (lo, hi) in enumerate(((0, H), (H, PICKS))):
+        E.wait_ge(S["hq%d" % n], 1)
+        E.wait_ge(S["rb%d" % n], 1)
+        bank = 4 + n
+        src, out = T.ps[:, 512 * bank:512 * bank + hi - lo], T.ys[:, lo:hi]
+        E.matmul_mx(src, T.vq[:], T.vp[:], T.hq[:, lo:hi], T.hp[:, lo:hi], True, True).then_inc(S["my%d" % n], 1)
+        if n == 0:
+            A.wait_ge(S["my%d" % n], 1)
+            A.activation(out, src, COPY).then_inc(S["cy%d" % n], 1)
+        else:
+            V.wait_ge(S["my%d" % n], 1)
+            V.tensor_copy(out, src).then_inc(S["cy%d" % n], 1)
+        Y.wait_ge(S["cy%d" % n], 1)
+        Y.dma_start(T.y[:, lo:hi], T.ys[:, lo:hi]).then_inc(S["out%d" % n], 16)
+    for n in range(2):
+        Y.wait_ge(S["out%d" % n], 16)

@@ -3,6 +3,7 @@ from concourse.mybir import dt, AluOpType, ActivationFunctionType
 
 N, W, CAP, PICKS = 8, 512, 64, 512
 PAD = 16
+BS = (0, 2, 1, 3)
 CODES, BYTE = "float8_e4m3fn_x4", "uint8"
 SCRATCH = {
     "lst": ("sbuf", [128, 32], "int32"),
@@ -29,8 +30,8 @@ SCRATCH = {
 for _t in range(4):
     SCRATCH["off%d" % _t] = ("sbuf", [128, 32], "uint16")
     SCRATCH["res%d" % _t] = ("sbuf", [128, W + N * CAP], "bfloat16")
-SEMAPHORES = (["lst", "xin", "pkin", "win", "vin", "pad", "wqd", "xqd", "vqd", "pkd", "loc"]
-              + [k + "%d" % i for k in ("off", "gat", "sqd", "fill", "mo", "ro", "ms", "rs", "hg", "hq", "my", "cy", "out",
+SEMAPHORES = (["lst", "xin", "pkin", "win", "vin", "pad", "xqd", "vqd", "pkd", "loc"]
+              + [k + "%d" % i for k in ("wqd", "off", "gat", "sqd", "fill", "mo", "ro", "rs", "hg", "hq", "my", "cy", "out",
                                         "arr", "ma", "mb", "mc", "ra", "rb", "rc") for i in range(4)])
 
 
@@ -109,7 +110,7 @@ def rank_program(g, core, T, topo):
         pieces.append((runs, lo, col))
 
     for q in range(8):
-        (Y if q < 3 else A).dma_start(T.lst[16 * q:16 * q + 16, :], T.snd[:, :]).then_inc(S.lst, 16)
+        (Y if q < 4 else A).dma_start(T.lst[16 * q:16 * q + 16, :], T.snd[:, :]).then_inc(S.lst, 16)
     Y.dma_start(T.xs[:, PAD:PAD + 4 * W], T.x[:, :]).then_inc(S.xin, 16)
     Y.dma_start(T.ws[:], T.w[:, :]).then_inc(S.win, 16)
     Y.dma_start(T.pkl[:], T.pk[:, :]).then_inc(S.pkin, 16)
@@ -122,7 +123,7 @@ def rank_program(g, core, T, topo):
     for b in range(4):
         V.memset(T["res%d" % b][:, W + CAP * rank:W + CAP * rank + CAP], 0.0).then_inc(S["fill%d" % b], 1)
 
-    for q, ts in ((V, (0, 1)), (A, (2, 3))):
+    for q, ts in ((V, (0, 1)), (A, (2, 3, 1))):
         q.wait_ge(S.pad, 1)
         q.wait_ge(S.xin, 16)
         for t in ts:
@@ -134,19 +135,22 @@ def rank_program(g, core, T, topo):
             for d0, d1, c in runs:
                 out = T.gath[:, 4 * c + t:4 * (c + CAP * (d1 - d0)):4]
                 src = T.xs[:, 0:PAD + 4 * W].indirect(T["off%d" % t][:, 4 * d0:4 * d1])
-                if t < 2:
+                if t < (2, 1, 2)[k]:
                     V.tensor_copy(out, src).then_inc(S["gat%d" % k], 1)
                 else:
                     A.activation(out, src, COPY).then_inc(S["gat%d" % k], 1)
         V.wait_ge(S["gat%d" % k], 4 * len(runs))
         V.quantize_mx(T.sq[:, lo:hi], T.sp[:, lo:hi], T.gath[:, 4 * lo:4 * hi]).then_inc(S["sqd%d" % k], 1)
+        if k == 0:
+            V.quantize_mx(T.cq[:, 0:W], T.cp[:, 0:W], T.xs[:, PAD:PAD + 4 * W]).then_inc(S.xqd, 1)
         g.wait_ge(S["sqd%d" % k], 1)
         sent += send(g, core, rank, dests, at, T, topo)
     g.wait_ge(S.loc, sent)
 
     V.wait_ge(S.win, 16)
-    V.quantize_mx(T.wq[:], T.wp[:], T.ws[:]).then_inc(S.wqd, 1)
-    V.quantize_mx(T.cq[:, 0:W], T.cp[:, 0:W], T.xs[:, PAD:PAD + 4 * W]).then_inc(S.xqd, 1)
+    for b in BS:
+        V.quantize_mx(T.wq[:, 128 * b:128 * b + 128], T.wp[:, 128 * b:128 * b + 128],
+                      T.ws[:, 512 * b:512 * b + 512]).then_inc(S["wqd%d" % b], 1)
     V.wait_ge(S.vin, 16)
     V.quantize_mx(T.vq[:], T.vp[:], T.vs[:]).then_inc(S.vqd, 1)
     V.wait_ge(S.pkin, 16)
@@ -165,25 +169,7 @@ def rank_program(g, core, T, topo):
         else:
             A.activation(out, src, RELU, scale=0.05).then_inc(S["%s%d" % (done, b)], 1)
 
-    BS = (0, 2, 1, 3)
-    E.wait_ge(S.wqd, 1)
-    E.wait_ge(S.xqd, 1)
-    for b in BS:
-        product(b, b, 0, W, "mo")
-        keep(b, b, 0, 0, W, "mo", "ro")
-    away = topo.engines(core, T.cores[groups[mine - 1][0]])
-    E.wait_ge(S["arr%d" % mine], 2 * len(away))
-    for b in BS:
-        product(b, 4 + b, W - CAP, W + CAP, "ms")
-        keep(b, 4 + b, CAP, W + CAP * mate, CAP, "ms", "rs")
-    for n, i in enumerate(ring(rank, -1, T, topo)):
-        E.wait_ge(S["arr%d" % i], 2 * len(away))
-        lo = W + CAP + 2 * CAP * n
-        for b in BS:
-            bank = (0, 4, 0)[n] + b
-            E.wait_ge(S["%s%d" % (("ro", "rs", "ra")[n], b)], 1)
-            product(b, bank, lo, lo + 2 * CAP, ("ma", "mb", "mc")[n])
-            keep(b, bank, 0, W + CAP * groups[i][0], 2 * CAP, ("ma", "mb", "mc")[n], ("ra", "rb", "rc")[n])
+    H, M = 320, 448
 
     def ready(q, b):
         for k in ("fill", "ro", "rs", "ra", "rb", "rc"):
@@ -197,13 +183,32 @@ def rank_program(g, core, T, topo):
         else:
             A.activation(out, idx, COPY).then_inc(done, 1)
 
-    H, M = 320, 416
+    E.wait_ge(S.xqd, 1)
+    for b in BS:
+        E.wait_ge(S["wqd%d" % b], 1)
+        product(b, b, 0, W, "mo")
+        keep(b, b, 0, 0, W, "mo", "ro")
+    away = topo.engines(core, T.cores[groups[mine - 1][0]])
+    E.wait_ge(S["arr%d" % mine], 2 * len(away))
     V.wait_ge(S.pkd, 1)
     A.wait_ge(S.pkd, 1)
-    for q, bs in ((V, (0, 1)), (A, (2, 3))):
-        for b in bs:
-            ready(q, b)
-            pick(q, b, 0, H, S.hg0)
+    for n, i in enumerate(ring(rank, -1, T, topo)):
+        E.wait_ge(S["arr%d" % i], 2 * len(away))
+        lo, skip = W + CAP + 2 * CAP * n, 0 if n else CAP
+        made, done = ("ma", "mb", "mc")[n], ("ra", "rb", "rc")[n]
+        for b in BS:
+            bank = (4, 0, 4)[n] + b
+            for k in ((), ("ro",), ("rs", "ra"))[n]:
+                E.wait_ge(S["%s%d" % (k, b)], 1)
+            product(b, bank, lo - skip, lo + 2 * CAP, made)
+            if n == 0:
+                keep(b, bank, 0, W + CAP * mate, CAP, made, "rs")
+            keep(b, bank, skip, W + CAP * groups[i][0], 2 * CAP, made, done)
+            if n == 2:
+                q = V if b < 2 else A
+                ready(q, b)
+                pick(q, b, 0, H, S.hg0)
+
     pick(V, 0, H, PICKS, S.hg1)
     V.wait_ge(S.hg0, 4)
     V.quantize_mx(T.hq[:, 0:H], T.hp[:, 0:H], T.h[:, 0:4 * H]).then_inc(S.hq0, 1)
@@ -218,14 +223,13 @@ def rank_program(g, core, T, topo):
     for n, (lo, hi) in enumerate(((0, H), (H, PICKS))):
         E.wait_ge(S["hq%d" % n], 1)
         E.wait_ge(S["rb%d" % n], 1)
-        bank = 4 + n
-        src, out = T.ps[:, 512 * bank:512 * bank + hi - lo], T.ys[:, lo:hi]
+        src, out = T.ps[:, 512 * n:512 * n + hi - lo], T.ys[:, lo:hi]
         E.matmul_mx(src, T.vq[:], T.vp[:], T.hq[:, lo:hi], T.hp[:, lo:hi], True, True).then_inc(S["my%d" % n], 1)
-        if n == 0:
-            A.wait_ge(S["my%d" % n], 1)
+        q = (A, V)[n]
+        q.wait_ge(S["my%d" % n], 1)
+        if q is A:
             A.activation(out, src, COPY).then_inc(S["cy%d" % n], 1)
         else:
-            V.wait_ge(S["my%d" % n], 1)
             V.tensor_copy(out, src).then_inc(S["cy%d" % n], 1)
         Y.wait_ge(S["cy%d" % n], 1)
         Y.dma_start(T.y[:, lo:hi], T.ys[:, lo:hi]).then_inc(S["out%d" % n], 16)

from concourse.bass import DstId, RemoteDMATransfer
from concourse.mybir import dt, AluOpType, ActivationFunctionType

N, W, CAP, PICKS = 8, 512, 64, 512
PAD = 16
BS = (0, 2, 1, 3)
CODES, BYTE = "float8_e4m3fn_x4", "uint8"
SCRATCH = {
    "lst": ("sbuf", [128, 32], "int32"),
    "pkl": ("sbuf", [128, 32], "int32"),
    "pko": ("sbuf", [128, 32], "uint16"),
    "xs": ("sbuf", [128, PAD + 4 * W], "bfloat16"),
    "ws": ("sbuf", [128, 2048], "bfloat16"),
    "vs": ("sbuf", [128, 512], "bfloat16"),
    "gath": ("sbuf", [128, 4 * 7 * CAP], "bfloat16"),
    "sq": ("sbuf", [128, 7 * CAP], CODES),
    "sp": ("sbuf", [128, 7 * CAP], BYTE),
    "cq": ("sbuf", [128, W + 7 * CAP], CODES),
    "cp": ("sbuf", [128, W + 7 * CAP], BYTE),
    "wq": ("sbuf", [128, 512], CODES),
    "wp": ("sbuf", [128, 512], BYTE),
    "vq": ("sbuf", [128, 128], CODES),
    "vp": ("sbuf", [128, 128], BYTE),
    "h": ("sbuf", [128, 4 * PICKS], "bfloat16"),
    "hq": ("sbuf", [128, PICKS], CODES),
    "hp": ("sbuf", [128, PICKS], BYTE),
    "ys": ("sbuf", [128, PICKS], "float32"),
    "ps": ("psum", [128, 4096], "float32"),
}
for _t in range(4):
    SCRATCH["off%d" % _t] = ("sbuf", [128, 32], "uint16")
    SCRATCH["res%d" % _t] = ("sbuf", [128, W + N * CAP], "bfloat16")
SEMAPHORES = (["lst", "xin", "pkin", "win", "vin", "pad", "xqd", "vqd", "pkd", "loc"]
              + [k + "%d" % i for k in ("wqd", "off", "gat", "sqd", "fill", "mo", "ro", "rs", "hg", "hq", "my", "cy", "out",
                                        "arr", "ma", "mb", "mc", "ra", "rb", "rc") for i in range(4)])


def mask_of(engines):
    return sum(1 << e for e in engines)


def groups_of(T, topo):
    out = {}
    for r, c in enumerate(T.cores):
        out.setdefault(topo.chip(c), []).append(r)
    return [out[k] for k in sorted(out, key=lambda k: out[k][0])]


def ring(rank, step, T, topo):
    groups = groups_of(T, topo)
    mine = [i for i, q in enumerate(groups) if rank in q][0]
    around = [(mine + step * k) % len(groups) for k in range(1, len(groups))]
    near = [i for i in around if topo.same_plane(topo.chip(T.cores[rank]), topo.chip(T.cores[groups[i][0]]))]
    return [i for i in around if i not in near] + near


def place(dst, src, T, topo):
    groups = groups_of(T, topo)
    i = [n for n, q in enumerate(groups) if src in q][0]
    if dst in groups[i]:
        return W, i
    return W + CAP + 2 * CAP * ring(dst, -1, T, topo).index(i) + CAP * groups[i].index(src), i


def send(g, core, me, dests, at, T, topo):
    far = [d for d in dests if topo.chip(T.cores[d]) != topo.chip(core)]
    away = topo.engines(core, T.cores[far[0]])
    share, total = len(away) // len(far), 0
    for buf, land in (("sq", "cq"), ("sp", "cp")):
        trs = []
        for d in dests:
            if d in far:
                k = far.index(d)
                eng = away[k * share:(k + 1) * share]
            else:
                eng = [e for e in topo.engines(core, T.cores[d]) if e not in away][:len(away)]
            col, i = place(d, me, T, topo)
            a, b = T[buf][:, at[d]:at[d] + CAP], T[land][:, col:col + CAP]
            if buf == "sq":
                a, b = a.bitcast(dt.uint8), b.bitcast(dt.uint8)
            rid, pid, _ = topo.addr(T.cores[d])
            trs.append(RemoteDMATransfer(dst_ids=[DstId(rid=rid, pnc=pid)], dma_engine_mask=mask_of(eng),
                                         remote_sem=T.sem["arr%d" % i], src=a, dst=b))
            total += len(eng)
        g.remote_dma_fused(trs, local_sem=T.sem.loc)
    return total


def rank_program(g, core, T, topo):
    rank = T.rank_of(core)
    if rank is None:
        return
    S, V, A, E, Y = T.sem, g.vector, g.scalar, g.tensor, g.sync
    COPY, RELU = ActivationFunctionType.Copy, ActivationFunctionType.Relu
    groups = groups_of(T, topo)
    mine = [i for i, q in enumerate(groups) if rank in q][0]
    mate = [d for d in groups[mine] if d != rank][0]
    steps = [list(groups[i]) for i in ring(rank, 1, T, topo)]
    steps[1].append(mate)
    at, pieces, col = {}, [], 0
    for dests in steps:
        runs, lo = [], col
        for d in sorted(dests):
            at[d] = col
            if runs and runs[-1][1] == d:
                runs[-1][1] = d + 1
            else:
                runs.append([d, d + 1, col])
            col += CAP
        pieces.append((runs, lo, col))

    for q in range(8):
        (Y if q < 4 else A).dma_start(T.lst[16 * q:16 * q + 16, :], T.snd[:, :]).then_inc(S.lst, 16)
    Y.dma_start(T.xs[:, PAD:PAD + 4 * W], T.x[:, :]).then_inc(S.xin, 16)
    Y.dma_start(T.ws[:], T.w[:, :]).then_inc(S.win, 16)
    Y.dma_start(T.pkl[:], T.pk[:, :]).then_inc(S.pkin, 16)
    Y.dma_start(T.vs[:], T.v[:, :]).then_inc(S.vin, 16)

    V.memset(T.xs[:, 0:PAD], 0.0).then_inc(S.pad, 1)
    V.wait_ge(S.lst, 128)
    for t in (2, 0, 3, 1):
        V.tensor_scalar(T["off%d" % t][:], T.lst[:], 4.0, float(PAD + t), AluOpType.mult, AluOpType.add).then_inc(S["off%d" % t], 1)
    for b in range(4):
        V.memset(T["res%d" % b][:, W + CAP * rank:W + CAP * rank + CAP], 0.0).then_inc(S["fill%d" % b], 1)

    for q, ts in ((V, (0, 1)), (A, (2, 3, 1))):
        q.wait_ge(S.pad, 1)
        q.wait_ge(S.xin, 16)
        for t in ts:
            q.wait_ge(S["off%d" % t], 1)
    sent = 0
    for k, dests in enumerate(steps):
        runs, lo, hi = pieces[k]
        for t in range(4):
            for d0, d1, c in runs:
                out = T.gath[:, 4 * c + t:4 * (c + CAP * (d1 - d0)):4]
                src = T.xs[:, 0:PAD + 4 * W].indirect(T["off%d" % t][:, 4 * d0:4 * d1])
                if t < (2, 1, 2)[k]:
                    V.tensor_copy(out, src).then_inc(S["gat%d" % k], 1)
                else:
                    A.activation(out, src, COPY).then_inc(S["gat%d" % k], 1)
        V.wait_ge(S["gat%d" % k], 4 * len(runs))
        V.quantize_mx(T.sq[:, lo:hi], T.sp[:, lo:hi], T.gath[:, 4 * lo:4 * hi]).then_inc(S["sqd%d" % k], 1)
        if k == 0:
            V.quantize_mx(T.cq[:, 0:W], T.cp[:, 0:W], T.xs[:, PAD:PAD + 4 * W]).then_inc(S.xqd, 1)
        g.wait_ge(S["sqd%d" % k], 1)
        sent += send(g, core, rank, dests, at, T, topo)
    g.wait_ge(S.loc, sent)

    V.wait_ge(S.win, 16)
    for b in BS:
        V.quantize_mx(T.wq[:, 128 * b:128 * b + 128], T.wp[:, 128 * b:128 * b + 128],
                      T.ws[:, 512 * b:512 * b + 512]).then_inc(S["wqd%d" % b], 1)
    V.wait_ge(S.vin, 16)
    V.quantize_mx(T.vq[:], T.vp[:], T.vs[:]).then_inc(S.vqd, 1)
    V.wait_ge(S.pkin, 16)
    V.tensor_copy(T.pko[:], T.pkl[:]).then_inc(S.pkd, 1)

    def product(b, bank, lo, hi, done):
        E.matmul_mx(T.ps[:, 512 * bank:512 * bank + hi - lo], T.wq[:, 128 * b:128 * b + 128], T.wp[:, 128 * b:128 * b + 128],
                    T.cq[:, lo:hi], T.cp[:, lo:hi], True, True).then_inc(S["%s%d" % (done, b)], 1)

    def keep(b, bank, skip, lo, n, made, done):
        q = V if b < 2 else A
        q.wait_ge(S["%s%d" % (made, b)], 1)
        src, out = T.ps[:, 512 * bank + skip:512 * bank + skip + n], T["res%d" % b][:, lo:lo + n]
        if b < 2:
            V.tensor_scalar(out, src, 0.0, 0.05, AluOpType.max, AluOpType.mult).then_inc(S["%s%d" % (done, b)], 1)
        else:
            A.activation(out, src, RELU, scale=0.05).then_inc(S["%s%d" % (done, b)], 1)

    H, M = 320, 448

    def ready(q, b):
        for k in ("fill", "ro", "rs", "ra", "rb", "rc"):
            q.wait_ge(S["%s%d" % (k, b)], 1)

    def pick(q, b, lo, hi, done):
        out = T.h[:, 4 * lo + b:4 * hi:4]
        idx = T["res%d" % b][:, 0:W + N * CAP].indirect(T.pko[:, lo // 16:hi // 16])
        if q is V:
            V.tensor_copy(out, idx).then_inc(done, 1)
        else:
            A.activation(out, idx, COPY).then_inc(done, 1)

    E.wait_ge(S.xqd, 1)
    for b in BS:
        E.wait_ge(S["wqd%d" % b], 1)
        product(b, b, 0, W, "mo")
        keep(b, b, 0, 0, W, "mo", "ro")
    away = topo.engines(core, T.cores[groups[mine - 1][0]])
    E.wait_ge(S["arr%d" % mine], 2 * len(away))
    V.wait_ge(S.pkd, 1)
    A.wait_ge(S.pkd, 1)
    for n, i in enumerate(ring(rank, -1, T, topo)):
        E.wait_ge(S["arr%d" % i], 2 * len(away))
        lo, skip = W + CAP + 2 * CAP * n, 0 if n else CAP
        made, done = ("ma", "mb", "mc")[n], ("ra", "rb", "rc")[n]
        for b in BS:
            bank = (4, 0, 4)[n] + b
            for k in ((), ("ro",), ("rs", "ra"))[n]:
                E.wait_ge(S["%s%d" % (k, b)], 1)
            product(b, bank, lo - skip, lo + 2 * CAP, made)
            if n == 0:
                keep(b, bank, 0, W + CAP * mate, CAP, made, "rs")
            keep(b, bank, skip, W + CAP * groups[i][0], 2 * CAP, made, done)
            if n == 2:
                q = V if b < 2 else A
                ready(q, b)
                pick(q, b, 0, H, S.hg0)

    pick(V, 0, H, PICKS, S.hg1)
    V.wait_ge(S.hg0, 4)
    V.quantize_mx(T.hq[:, 0:H], T.hp[:, 0:H], T.h[:, 0:4 * H]).then_inc(S.hq0, 1)
    pick(V, 1, H, M, S.hg1)
    pick(A, 2, H, PICKS, S.hg1)
    pick(A, 3, H, PICKS, S.hg1)
    ready(A, 1)
    pick(A, 1, M, PICKS, S.hg1)
    V.wait_ge(S.hg1, 5)
    V.quantize_mx(T.hq[:, H:PICKS], T.hp[:, H:PICKS], T.h[:, 4 * H:4 * PICKS]).then_inc(S.hq1, 1)
    E.wait_ge(S.vqd, 1)
    for n, (lo, hi) in enumerate(((0, H), (H, PICKS))):
        E.wait_ge(S["hq%d" % n], 1)
        E.wait_ge(S["rb%d" % n], 1)
        src, out = T.ps[:, 512 * n:512 * n + hi - lo], T.ys[:, lo:hi]
        E.matmul_mx(src, T.vq[:], T.vp[:], T.hq[:, lo:hi], T.hp[:, lo:hi], True, True).then_inc(S["my%d" % n], 1)
        q = (A, V)[n]
        q.wait_ge(S["my%d" % n], 1)
        if q is A:
            A.activation(out, src, COPY).then_inc(S["cy%d" % n], 1)
        else:
            V.tensor_copy(out, src).then_inc(S["cy%d" % n], 1)
        Y.wait_ge(S["cy%d" % n], 1)
        Y.dma_start(T.y[:, lo:hi], T.ys[:, lo:hi]).then_inc(S["out%d" % n], 16)
    for n in range(2):
        Y.wait_ge(S["out%d" % n], 16)
